import numpy as np
import ml_dtypes


def mxq(x, axis, fmt="e4m3"):
    dtype, down = {"e4m3": (ml_dtypes.float8_e4m3fn, 7), "e5m2": (ml_dtypes.float8_e5m2, 14)}[fmt]
    v = np.moveaxis(np.asarray(x, np.float32).astype(ml_dtypes.bfloat16).astype(np.float64), axis, -1)
    blocks = v.reshape(v.shape[:-1] + (-1, 32))
    amax = np.abs(blocks).max(-1, keepdims=True)
    byte = np.maximum(np.where(amax > 0, np.frexp(amax)[1] - 1 + 127, 0) - down, 1)
    scale = np.exp2(byte - 127.0)
    codes = (blocks / scale).astype(np.float32).astype(dtype).astype(np.float64)
    return np.moveaxis((codes * scale).reshape(v.shape), -1, axis)


WIDE = False


def mx_kscale(k):
    if not WIDE:
        return np.ones(k)
    levels = np.array([10, -10, 5, -5, 0])
    if k % 512:
        return np.exp2(np.random.permutation(np.resize(levels, k // 32))).repeat(32)
    a = np.empty((k // 512, 16))
    for p in range(k // 512):
        a[p, :8] = np.random.permutation(np.resize(levels, 8))
        for g in range(8):
            far = levels[np.abs(levels - a[p, g]) >= 10]
            a[p, g + 8] = far[np.random.randint(len(far))]
    return np.exp2(a.ravel()).repeat(32)


BF16 = ml_dtypes.bfloat16


def bf(x):
    return np.asarray(x, np.float32).astype(BF16)


def f64(x):
    return np.asarray(x).astype(np.float64)


E2M1 = np.array([0.0, 0.5, 1.0, 1.5, 2.0, 3.0, 4.0, 6.0, -0.0, -0.5, -1.0, -1.5, -2.0, -3.0, -4.0, -6.0])


def pack_weight(w, fmt):
    k, n = w.shape
    w = f64(bf(w)).reshape(k // 32, 32, n)
    amax = np.abs(w).max(1)
    if fmt == "e4m3":
        byte = np.frexp(amax)[1] - 1 + 127 - 7
    else:
        mant, ex = np.frexp(amax / 6.0)
        byte = np.where(mant > 0.5, ex, ex - 1) + 127
    byte = np.clip(np.where(amax > 0, byte, 1), 1, 254)
    scaled = (w * np.exp2(127.0 - byte)[:, None, :]).reshape(k, n).astype(np.float32)
    by_word = np.ascontiguousarray(scaled.reshape(k // 512, 128, 4, n).transpose(0, 1, 3, 2))
    if fmt == "e4m3":
        words = by_word.astype(ml_dtypes.float8_e4m3fn).view(np.uint8)
    else:
        c = by_word.astype(ml_dtypes.float4_e2m1fn).view(np.uint8) & 0xF
        words = c[..., 0::2] | (c[..., 1::2] << 4)
    return np.ascontiguousarray(words), np.ascontiguousarray(byte.astype(np.uint8).reshape(k // 512, 16, n))


def unpack_weight(words, scales, fmt):
    g, p, n, _ = words.shape
    if fmt == "e4m3":
        vals = np.ascontiguousarray(words).view(ml_dtypes.float8_e4m3fn).astype(np.float64)
    else:
        nib = np.empty((g, p, n, 4), np.uint8)
        nib[..., 0::2] = words & 0xF
        nib[..., 1::2] = words >> 4
        vals = E2M1[nib]
    vals = vals * np.repeat(np.exp2(scales.astype(np.float64) - 127.0), 8, axis=1)[..., None]
    return vals.transpose(0, 1, 3, 2).reshape(g * 512, n)
def pack4(w):
    words, scales = pack_weight(w, "e2m1")
    return words.reshape(words.shape[0], 128, -1), scales


def unpack4(words, scales):
    return unpack_weight(words.reshape(words.shape[0], 128, -1, 2), scales, "e2m1")


def planes(Y):
    n, m = Y.shape
    b = f64(bf(Y)).reshape(n // 32, 32, m)
    amax = np.abs(b).max(1)
    byte = np.clip(np.where(amax > 0, np.frexp(amax)[1] - 1 + 127 - 7, 1), 1, 254)
    codes = (b * np.exp2(127.0 - byte)[:, None, :]).reshape(n, m).astype(np.float32).astype(ml_dtypes.float8_e4m3fn).view(np.uint8)
    words = codes.reshape(n // 512, 128, 4, m).transpose(0, 1, 3, 2)
    return np.ascontiguousarray(words), np.ascontiguousarray(byte.astype(np.uint8).reshape(n // 512, 16, m))


G, P, W, F, T = 4, 256, 2048, 1024, 2048


def setup_inputs():
    s = mx_kscale(W)
    t = mx_kscale(F)
    assign = np.exp(np.random.randn(G, P, W) - 1.0)
    levels = np.random.randn(W, F) / np.sqrt(W)
    skill_weight = np.exp(0.3 * np.random.randn(F))
    required = np.random.randn(F, T) / np.sqrt(F)
    site_weight = np.exp(0.8 * np.random.randn(G, T))
    skill_words, skill_scales = pack4(levels * s[:, None])
    task_words, task_scales = pack4(required / t[:, None])
    return {"assign": bf(assign / s), "skill_words": skill_words, "skill_scales": skill_scales,
            "skill_weight": bf(skill_weight * t), "task_words": task_words, "task_scales": task_scales,
            "site_weight": bf(site_weight)}

def reference(assign, skill_words, skill_scales, skill_weight, task_words, task_scales, site_weight):
    A = f64(assign).reshape(G * P, W)
    L = unpack4(skill_words, skill_scales)
    R = unpack4(task_words, task_scales)
    Z = mxq(A, 1, "e4m3") @ L
    C = np.minimum(Z, 1.0) * f64(skill_weight)
    V = mxq(C, 1, "e4m3") @ R
    y = V.reshape(G, P, T) * f64(site_weight)[:, None, :]
    Y = y.reshape(G * P, T).T
    words, scales = planes(Y)
    return y, words, scales

@@ -1,0 +1,342 @@
+from contextlib import ExitStack
+
+import concourse.mybir as mybir
+from concourse.masks import make_identity
+
+G, SHIFTS, W, F, T = 4, 256, 2048, 1024, 2048
+ROWS = G * SHIFTS
+FLOPS = 2 * ROWS * W * F + 2 * ROWS * F * T
+
+F32 = mybir.dt.float32
+BF16 = mybir.dt.bfloat16
+I32 = mybir.dt.int32
+U32 = mybir.dt.uint32
+U8 = mybir.dt.uint8
+FP8X4 = mybir.dt.float8_e4m3fn_x4
+FP4X4 = mybir.dt.float4_e2m1fn_x4
+ALU = mybir.AluOpType
+
+P = 128
+BANK = 512
+TILES = ROWS // P
+W_PASSES = W // 512
+F_PASSES = F // 512
+T_GROUPS = T // 512
+BANKS = 8
+
+
+def tile_capped_skill_task_fit_h1_kernel(
+    tc, assign, skill_words, skill_scales, skill_weight, task_words, task_scales, site_weight, out_0, out_1, out_2
+):
+    nc = tc.nc
+    a_rows = assign.rearrange("s j w -> (s j) w")
+    y_rows = out_0.rearrange("s j d -> (s j) d")
+    y_words = out_1.rearrange("g p m t -> p g (m t)").bitcast(I32)
+
+    with ExitStack() as ctx:
+        keep = ctx.enter_context(tc.tile_pool(name="keep", bufs=1))
+        psum = ctx.enter_context(tc.psum_pool(name="psum", bufs=1))
+        ctx.enter_context(tc.manual_schedule())
+
+        def ring(label, count, shape, dtype):
+            return [keep.tile(shape, dtype, name="%s%d" % (label, n), align_bytes=64) for n in range(count)]
+
+        banks = [psum.tile([P, BANK], F32, name="bank%d" % n) for n in range(BANKS)]
+        bank_uses = []
+
+        def take_bank():
+            bank_uses.append(None)
+            return banks[(len(bank_uses) - 1) % BANKS]
+
+        ident = keep.tile([P, P], F32, name="ident", align_bytes=64)
+        skill_col = keep.tile([P, F // P], BF16, name="skill_col", align_bytes=64)
+        site_col = keep.tile([P, G, T // P], BF16, name="site_col", align_bytes=64)
+        skill_all = keep.tile([P, F], BF16, name="skill_all", align_bytes=64)
+        site_all = ring("site_all", G, [P, T], BF16)
+        l_words = ring("l_words", W_PASSES, [P, 2 * F], U8)
+        r_words = ring("r_words", F_PASSES, [P, 2 * T], U8)
+        l_scales = keep.tile([P, W_PASSES, F], U8, name="l_scales", align_bytes=64)
+        r_scales = keep.tile([P, F_PASSES, T], U8, name="r_scales", align_bytes=64)
+        a_raw = ring("a_raw", TILES, [P, W], BF16)
+        a_split = ring("a_split", 2, [P, 2, 2, W // 8], F32)
+        a_grouped = ring("a_grouped", 2, [P, W], BF16)
+        a_codes = ring("a_codes", 3, [P, W // 4], U32)
+        a_scales = ring("a_scales", 3, [P, W // 4], U8)
+        c_split = ring("c_split", 2, [P, F], BF16)
+        c_grouped = ring("c_grouped", 2, [P, F], BF16)
+        c_codes = ring("c_codes", 3, [P, F // 4], U32)
+        c_scales = ring("c_scales", 3, [P, F // 4], U8)
+        y_f32 = ring("y_f32", 4, [P, T], F32)
+        y_split = ring("y_split", 2, [P, T], BF16)
+        y_grouped = ring("y_grouped", 2, [P, T], BF16)
+        y_codes = keep.tile([P, T_GROUPS, ROWS], U32, name="y_codes", align_bytes=64)
+        y_scales = keep.tile([P, T_GROUPS, ROWS], U8, name="y_scales", align_bytes=64)
+
+        def pick(tiles, i):
+            return tiles[i % len(tiles)]
+
+        def load_a(i, lo, hi):
+            nc.sync.dma_start(out=a_raw[i][:, lo:hi], in_=a_rows[i * P : (i + 1) * P, lo:hi])
+
+        def load_scales(plane, rows):
+            for q in range(4):
+                nc.gpsimd.dma_start(
+                    out=plane[32 * q : 32 * q + 4, :, :].bitcast(I32),
+                    in_=rows[:, 4 * q : 4 * q + 4, :].rearrange("g r n -> r g n").bitcast(I32),
+                )
+
+        nc.vector.memset(l_scales[:].bitcast(I32), 0)
+        nc.vector.memset(r_scales[:].bitcast(I32), 0)
+        make_identity(nc, ident[:])
+        nc.scalar.dma_start(out=skill_col[:], in_=skill_weight.rearrange("(p c) -> p c", p=P))
+        nc.scalar.dma_start(out=site_col[:], in_=site_weight.rearrange("s (p c) -> p s c", p=P))
+        load_a(0, 0, W // 2)
+        load_a(0, W // 2, W)
+        load_a(1, 0, W)
+        load_scales(l_scales, skill_scales)
+        for g in range(W_PASSES):
+            nc.sync.dma_start(out=l_words[g][:].bitcast(I32), in_=skill_words[g].bitcast(I32))
+        load_a(2, 0, W)
+        load_scales(r_scales, task_scales)
+        for g in range(F_PASSES):
+            nc.sync.dma_start(out=r_words[g][:].bitcast(I32), in_=task_words[g].bitcast(I32))
+        for i in range(3, TILES):
+            load_a(i, 0, W)
+
+        def spread(columns, dst):
+            bank = take_bank()
+            for j in range(4):
+                nc.tensor.transpose(bank[:, j * P : (j + 1) * P], columns[:, j : j + 1].to_broadcast([P, P]), ident[:])
+            nc.scalar.copy(out=dst, in_=bank[:].rearrange("p (j q) -> p q j", j=4))
+
+        def spread_skill():
+            spread(skill_col[:].bitcast(F32), skill_all[:].bitcast(F32).rearrange("p (q j) -> p q j", j=4))
+
+        def spread_site(s, h):
+            spread(
+                site_col[:, s, :].bitcast(F32)[:, 4 * h : 4 * h + 4],
+                site_all[s][:].bitcast(F32).rearrange("p (q h j) -> p h q j", h=2, j=4)[:, h],
+            )
+
+        def turn(sources, dst, engine_copy):
+            bank = take_bank()
+            n = len(sources)
+            for c in range(n):
+                nc.tensor.transpose(bank[:, c * P : (c + 1) * P], sources[c], ident[:])
+            engine_copy(
+                out=dst.bitcast(F32).rearrange("p (g r u) -> p g r u", r=P, u=2),
+                in_=bank[:, : n * P].rearrange("p (g u r) -> p g r u", r=P, u=2),
+            )
+
+        def split_a(i, halves):
+            words = a_raw[i][:].bitcast(F32).rearrange("p (h q u) -> p h u q", h=2, u=2)
+            nc.vector.tensor_copy(out=pick(a_split, i)[:, halves], in_=words[:, halves])
+
+        def turn_a(i, h):
+            src = pick(a_split, i)
+            turn(
+                [src[:, h, u, g * P : (g + 1) * P] for g in range(2) for u in range(2)],
+                pick(a_grouped, i)[:, h * 1024 : (h + 1) * 1024],
+                nc.scalar.copy,
+            )
+
+        def quantise(codes, scales, grouped):
+            nc.vector.quantize_mx(out=codes.bitcast(FP8X4), scales=scales, in_=grouped)
+
+        def quantise_a(i, lo, hi):
+            quantise(
+                pick(a_codes, i)[:, lo * P : hi * P],
+                pick(a_scales, i)[:, lo * P : hi * P],
+                pick(a_grouped, i)[:, lo * BANK : hi * BANK],
+            )
+
+        def z_pass(i, bank, half, g):
+            nc.tensor.matmul_mx(
+                out=bank[:],
+                lhsT=pick(a_codes, i)[:, g * P : (g + 1) * P].bitcast(FP8X4),
+                lhsT_scale=pick(a_scales, i)[:, g * P : (g + 1) * P],
+                rhs=l_words[g][:, half * 2 * BANK : (half + 1) * 2 * BANK].bitcast(FP4X4),
+                rhs_scale=l_scales[:, g, half * BANK : (half + 1) * BANK],
+                start=(g == 0),
+                stop=(g == W_PASSES - 1),
+            )
+
+        def z_product(i, half):
+            bank = take_bank()
+            for g in range(W_PASSES):
+                z_pass(i, bank, half, g)
+            return bank
+
+        def cap(i, half, bank):
+            z = bank[:].rearrange("p (q u e) -> p u q e", u=2, e=2)
+            weight = skill_all[:, half * BANK : (half + 1) * BANK].rearrange("p (q u e) -> p u q e", u=2, e=2)
+            c = pick(c_split, i)[:, half * BANK : (half + 1) * BANK].rearrange("p (u q e) -> p u q e", u=2, e=2)
+            for u in range(2):
+                nc.vector.scalar_tensor_tensor(
+                    out=c[:, u], in0=z[:, u], scalar=1.0, in1=weight[:, u], op0=ALU.min, op1=ALU.mult
+                )
+
+        def turn_c(i, engine_copy):
+            words = pick(c_split, i)[:].bitcast(F32)
+            turn([words[:, c * P : (c + 1) * P] for c in range(4)], pick(c_grouped, i)[:], engine_copy)
+
+        def quantise_c(i):
+            quantise(pick(c_codes, i)[:], pick(c_scales, i)[:], pick(c_grouped, i)[:])
+
+        def v_product(i, b):
+            bank = take_bank()
+            for g in range(F_PASSES):
+                nc.tensor.matmul_mx(
+                    out=bank[:],
+                    lhsT=pick(c_codes, i)[:, g * P : (g + 1) * P].bitcast(FP8X4),
+                    lhsT_scale=pick(c_scales, i)[:, g * P : (g + 1) * P],
+                    rhs=r_words[g][:, b * 2 * BANK : (b + 1) * 2 * BANK].bitcast(FP4X4),
+                    rhs_scale=r_scales[:, g, b * BANK : (b + 1) * BANK],
+                    start=(g == 0),
+                    stop=(g == F_PASSES - 1),
+                )
+            return bank
+
+        def weigh(i, b, bank):
+            cols = slice(b * BANK, (b + 1) * BANK)
+            nc.vector.tensor_tensor(
+                out=pick(y_f32, i)[:, cols], in0=bank[:], in1=site_all[i * P // SHIFTS][:, cols], op=ALU.mult
+            )
+
+        def round_y(i, b):
+            cols = slice(b * BANK, (b + 1) * BANK)
+            nc.scalar.copy(
+                out=pick(y_split, i)[:, cols].rearrange("p (u q e) -> p u q e", u=2, e=2),
+                in_=pick(y_f32, i)[:, cols].rearrange("p (q u e) -> p u q e", u=2, e=2),
+            )
+
+        def store_y(i, lo, hi):
+            cols = slice(lo * BANK, hi * BANK)
+            nc.sync.dma_start(out=y_rows[i * P : (i + 1) * P, cols], in_=pick(y_f32, i)[:, cols])
+
+        def turn_y(i, lo, hi, engine_copy):
+            words = pick(y_split, i)[:].bitcast(F32)
+            turn(
+                [words[:, c * P : (c + 1) * P] for c in range(2 * lo, 2 * hi)],
+                pick(y_grouped, i)[:, lo * BANK : hi * BANK],
+                engine_copy,
+            )
+
+        def quantise_y(i, lo, hi):
+            for g in range(lo, hi):
+                quantise(
+                    y_codes[:, g, i * P : (i + 1) * P],
+                    y_scales[:, g, i * P : (i + 1) * P],
+                    pick(y_grouped, i)[:, g * BANK : (g + 1) * BANK],
+                )
+
+        def store_codes(first, last, lo, hi):
+            nc.sync.dma_start(
+                out=y_words[:, lo:hi, first * P : last * P], in_=y_codes[:, lo:hi, first * P : last * P].bitcast(I32)
+            )
+
+        def store_scales(first, last, queues):
+            for q in range(4):
+                queues[q % len(queues)].dma_start(
+                    out=out_2[:, 4 * q : 4 * q + 4, first * P : last * P].rearrange("g r m -> r g m").bitcast(I32),
+                    in_=y_scales[32 * q : 32 * q + 4, :, first * P : last * P].bitcast(I32),
+                )
+
+        def v_stage(i, stores):
+            for b in range(T_GROUPS):
+                weigh(i, b, v_product(i, b))
+                round_y(i, b)
+                if (b + 1) % stores == 0:
+                    store_y(i, b + 1 - stores, b + 1)
+
+        spread_skill()
+        spread_site(0, 0)
+        split_a(0, slice(0, 1))
+        split_a(0, slice(1, 2))
+        turn_a(0, 0)
+        turn_a(0, 1)
+        spread_site(0, 1)
+        split_a(1, slice(0, 2))
+        quantise_a(0, 0, 2)
+        quantise_a(0, 2, 4)
+        turn_a(1, 0)
+        turn_a(1, 1)
+        first_banks = [take_bank(), take_bank()]
+        for g in range(W_PASSES):
+            for half in range(2):
+                z_pass(0, first_banks[half], half, g)
+        quantise_a(1, 0, 4)
+        split_a(2, slice(0, 2))
+        cap(0, 0, first_banks[0])
+        cap(0, 1, first_banks[1])
+
+        last = TILES - 1
+        for s in range(last):
+            if s > 0:
+                turn_c(s, nc.scalar.copy)
+            if 0 < s and s + 3 < TILES:
+                split_a(s + 3, slice(0, 2))
+            if s > 0:
+                quantise_c(s)
+            if s >= 3:
+                quantise_y(s - 3, 0, 4)
+                if s % 2 == 0:
+                    store_codes(s - 4, s - 2, 0, 4)
+            if s == last - 1:
+                store_scales(0, 4, [nc.sync])
+            if s + 2 < TILES:
+                turn_a(s + 2, 0)
+                turn_a(s + 2, 1)
+            if s == 0:
+                spread_site(1, 0)
+                turn_c(s, nc.scalar.copy)
+            if 1 <= s < last - 1:
+                round_y(s - 1, 3)
+            if s >= 2:
+                turn_y(s - 2, 0, 2, nc.scalar.copy)
+                turn_y(s - 2, 2, 4, nc.scalar.copy)
+            if s == last - 1:
+                round_y(s - 1, 3)
+            if 1 <= s <= 5:
+                spread_site((s + 2) // 2, s % 2)
+            if s + 2 < TILES:
+                quantise_a(s + 2, 0, 4)
+            if s == 0:
+                quantise_c(s)
+                split_a(3, slice(0, 2))
+            cap(s + 1, 0, z_product(s + 1, 0))
+            if s == last - 1:
+                quantise_y(s - 2, 0, 4)
+                store_codes(s - 2, s - 1, 0, 4)
+            cap(s + 1, 1, z_product(s + 1, 1))
+            for b in range(T_GROUPS):
+                weigh(s, b, v_product(s, b))
+                if b < 3:
+                    round_y(s, b)
+                if b % 2 == 1:
+                    store_y(s, b - 1, b + 1)
+
+        turn_c(last, nc.vector.tensor_copy)
+        round_y(last - 1, 3)
+        turn_y(last - 2, 0, 2, nc.scalar.copy)
+        quantise_c(last)
+        turn_y(last - 2, 2, 4, nc.vector.tensor_copy)
+        turn_y(last - 1, 0, 2, nc.scalar.copy)
+        turn_y(last - 1, 2, 4, nc.scalar.copy)
+        quantise_y(last - 2, 0, 4)
+        store_codes(last - 2, last - 1, 0, 4)
+        for b in range(T_GROUPS):
+            weigh(last, b, v_product(last, b))
+            round_y(last, b)
+            if b >= 1:
+                store_y(last, b if b > 1 else 0, b + 1)
+        quantise_y(last - 1, 0, 4)
+        store_codes(last - 1, last, 0, 4)
+        turn_y(last, 0, 2, nc.vector.tensor_copy)
+        turn_y(last, 2, 3, nc.scalar.copy)
+        turn_y(last, 3, 4, nc.scalar.copy)
+        quantise_y(last, 2, 3)
+        quantise_y(last, 0, 2)
+        quantise_y(last, 3, 4)
+        store_codes(last, last + 1, 0, 4)
+        store_scales(4, TILES, [nc.scalar, nc.sync])

@@ -79,11 +79,9 @@ def tile_capped_skill_task_fit_h1_kernel(
             nc.sync.dma_start(out=a_raw[i][:, lo:hi], in_=a_rows[i * P : (i + 1) * P, lo:hi])
 
         def load_scales(plane, rows):
-            for q in range(4):
-                nc.gpsimd.dma_start(
-                    out=plane[32 * q : 32 * q + 4, :, :].bitcast(I32),
-                    in_=rows[:, 4 * q : 4 * q + 4, :].rearrange("g r n -> r g n").bitcast(I32),
-                )
+            by_row = rows.rearrange("g (q r) n -> r q g n", r=4).bitcast(I32)
+            for r in range(4):
+                nc.sync.dma_start(out=plane[r:P:32, :, :].bitcast(I32), in_=by_row[r])
 
         nc.vector.memset(l_scales[:].bitcast(I32), 0)
         nc.vector.memset(r_scales[:].bitcast(I32), 0)
@@ -92,9 +90,10 @@ def tile_capped_skill_task_fit_h1_kernel(
         nc.scalar.dma_start(out=site_col[:], in_=site_weight.rearrange("s (p c) -> p s c", p=P))
         load_a(0, 0, W // 2)
         load_a(0, W // 2, W)
-        load_a(1, 0, W)
         load_scales(l_scales, skill_scales)
         for g in range(W_PASSES):
+            if g == 2:
+                load_a(1, 0, W)
             nc.sync.dma_start(out=l_words[g][:].bitcast(I32), in_=skill_words[g].bitcast(I32))
         load_a(2, 0, W)
         load_scales(r_scales, task_scales)
@@ -236,10 +235,11 @@ def tile_capped_skill_task_fit_h1_kernel(
             )
 
         def store_scales(first, last, queues):
-            for q in range(4):
-                queues[q % len(queues)].dma_start(
-                    out=out_2[:, 4 * q : 4 * q + 4, first * P : last * P].rearrange("g r m -> r g m").bitcast(I32),
-                    in_=y_scales[32 * q : 32 * q + 4, :, first * P : last * P].bitcast(I32),
+            by_row = out_2.rearrange("g (q r) m -> r q g m", r=4)
+            for r in range(4):
+                queues[r % len(queues)].dma_start(
+                    out=by_row[r][:, :, first * P : last * P].bitcast(I32),
+                    in_=y_scales[r:P:32, :, first * P : last * P].bitcast(I32),
                 )
 
         def v_stage(i, stores):
@@ -256,19 +256,29 @@ def tile_capped_skill_task_fit_h1_kernel(
         turn_a(0, 0)
         turn_a(0, 1)
         spread_site(0, 1)
-        split_a(1, slice(0, 2))
         quantise_a(0, 0, 2)
         quantise_a(0, 2, 4)
-        turn_a(1, 0)
-        turn_a(1, 1)
         first_banks = [take_bank(), take_bank()]
         for g in range(W_PASSES):
+            if g == 2:
+                split_a(1, slice(0, 2))
+                turn_a(1, 0)
+                turn_a(1, 1)
             for half in range(2):
                 z_pass(0, first_banks[half], half, g)
-        quantise_a(1, 0, 4)
         split_a(2, slice(0, 2))
+        quantise_a(1, 0, 4)
         cap(0, 0, first_banks[0])
         cap(0, 1, first_banks[1])
+
+        def v_bank(i, b):
+            weigh(i, b, v_product(i, b))
+            if b < 3 or i >= last - 1:
+                round_y(i, b)
+            if i == last:
+                store_y(i, b, b + 1)
+            elif b % 2 == 1:
+                store_y(i, b - 1, b + 1)
 
         last = TILES - 1
         for s in range(last):
@@ -278,65 +288,52 @@ def tile_capped_skill_task_fit_h1_kernel(
                 split_a(s + 3, slice(0, 2))
             if s > 0:
                 quantise_c(s)
-            if s >= 3:
-                quantise_y(s - 3, 0, 4)
-                if s % 2 == 0:
-                    store_codes(s - 4, s - 2, 0, 4)
-            if s == last - 1:
-                store_scales(0, 4, [nc.sync])
+            if s >= 2:
+                quantise_y(s - 2, 0, 4)
+                if s == last - 1:
+                    store_codes(s - 2, s - 1, 0, 4)
+                elif s % 2 == 1:
+                    store_codes(s - 3, s - 1, 0, 4)
             if s + 2 < TILES:
                 turn_a(s + 2, 0)
                 turn_a(s + 2, 1)
             if s == 0:
-                spread_site(1, 0)
                 turn_c(s, nc.scalar.copy)
-            if 1 <= s < last - 1:
+            if s >= 1:
                 round_y(s - 1, 3)
-            if s >= 2:
-                turn_y(s - 2, 0, 2, nc.scalar.copy)
-                turn_y(s - 2, 2, 4, nc.scalar.copy)
-            if s == last - 1:
-                round_y(s - 1, 3)
-            if 1 <= s <= 5:
-                spread_site((s + 2) // 2, s % 2)
-            if s + 2 < TILES:
-                quantise_a(s + 2, 0, 4)
+            cap(s + 1, 0, z_product(s + 1, 0))
             if s == 0:
                 quantise_c(s)
                 split_a(3, slice(0, 2))
-            cap(s + 1, 0, z_product(s + 1, 0))
-            if s == last - 1:
-                quantise_y(s - 2, 0, 4)
-                store_codes(s - 2, s - 1, 0, 4)
+            if s + 2 < TILES:
+                quantise_a(s + 2, 0, 4)
             cap(s + 1, 1, z_product(s + 1, 1))
+            if s >= 1:
+                turn_y(s - 1, 0, 2, nc.scalar.copy)
+                turn_y(s - 1, 2, 4, nc.scalar.copy)
+            if s <= 5:
+                spread_site((s + 2) // 2, s % 2)
             for b in range(T_GROUPS):
-                weigh(s, b, v_product(s, b))
-                if b < 3:
-                    round_y(s, b)
-                if b % 2 == 1:
-                    store_y(s, b - 1, b + 1)
+                v_bank(s, b)
 
         turn_c(last, nc.vector.tensor_copy)
-        round_y(last - 1, 3)
-        turn_y(last - 2, 0, 2, nc.scalar.copy)
+        quantise_y(last - 2, 0, 2)
         quantise_c(last)
-        turn_y(last - 2, 2, 4, nc.vector.tensor_copy)
+        quantise_y(last - 2, 2, 4)
+        store_codes(last - 2, last - 1, 0, 4)
+        store_scales(0, last - 1, [nc.sync])
         turn_y(last - 1, 0, 2, nc.scalar.copy)
         turn_y(last - 1, 2, 4, nc.scalar.copy)
-        quantise_y(last - 2, 0, 4)
-        store_codes(last - 2, last - 1, 0, 4)
-        for b in range(T_GROUPS):
-            weigh(last, b, v_product(last, b))
-            round_y(last, b)
-            if b >= 1:
-                store_y(last, b if b > 1 else 0, b + 1)
         quantise_y(last - 1, 0, 4)
         store_codes(last - 1, last, 0, 4)
+        for b in range(T_GROUPS):
+            v_bank(last, b)
         turn_y(last, 0, 2, nc.vector.tensor_copy)
-        turn_y(last, 2, 3, nc.scalar.copy)
+        turn_y(last, 2, 3, nc.vector.tensor_copy)
+        quantise_y(last, 0, 2)
         turn_y(last, 3, 4, nc.scalar.copy)
         quantise_y(last, 2, 3)
-        quantise_y(last, 0, 2)
+        store_codes(last, last + 1, 0, 3)
         quantise_y(last, 3, 4)
-        store_codes(last, last + 1, 0, 4)
-        store_scales(4, TILES, [nc.scalar, nc.sync])
+        store_codes(last, last + 1, 3, 4)
+        store_scales(last - 1, TILES, [nc.scalar, nc.sync])

@@ -50,7 +50,7 @@ def tile_capped_skill_task_fit_h1_kernel(
 
         ident = keep.tile([P, P], F32, name="ident", align_bytes=64)
         skill_col = keep.tile([P, F // P], BF16, name="skill_col", align_bytes=64)
-        site_col = keep.tile([P, G, T // P], BF16, name="site_col", align_bytes=64)
+        site_col = keep.tile([P, T // P], BF16, name="site_col", align_bytes=64)
         skill_all = keep.tile([P, F], BF16, name="skill_all", align_bytes=64)
         site_all = ring("site_all", G, [P, T], BF16)
         l_words = ring("l_words", W_PASSES, [P, 2 * F], U8)
@@ -78,6 +78,9 @@ def tile_capped_skill_task_fit_h1_kernel(
         def load_a(i, lo, hi):
             nc.sync.dma_start(out=a_raw[i][:, lo:hi], in_=a_rows[i * P : (i + 1) * P, lo:hi])
 
+        def load_site(s):
+            nc.sync.dma_start(out=site_all[s][:], in_=site_weight[s].partition_broadcast(P))
+
         def load_scales(plane, rows):
             by_row = rows.rearrange("g (q r) n -> r q g n", r=4).bitcast(I32)
             for r in range(4):
@@ -87,7 +90,7 @@ def tile_capped_skill_task_fit_h1_kernel(
         nc.vector.memset(r_scales[:].bitcast(I32), 0)
         make_identity(nc, ident[:])
         nc.scalar.dma_start(out=skill_col[:], in_=skill_weight.rearrange("(p c) -> p c", p=P))
-        nc.scalar.dma_start(out=site_col[:], in_=site_weight.rearrange("s (p c) -> p s c", p=P))
+        nc.scalar.dma_start(out=site_col[:], in_=site_weight[0].rearrange("(p c) -> p c", p=P))
         load_a(0, 0, W // 2)
         load_a(0, W // 2, W)
         load_scales(l_scales, skill_scales)
@@ -101,6 +104,7 @@ def tile_capped_skill_task_fit_h1_kernel(
             nc.sync.dma_start(out=r_words[g][:].bitcast(I32), in_=task_words[g].bitcast(I32))
         for i in range(3, TILES):
             load_a(i, 0, W)
+        load_site(1)
 
         def spread(columns, dst):
             bank = take_bank()
@@ -113,7 +117,7 @@ def tile_capped_skill_task_fit_h1_kernel(
 
         def spread_site(s, h):
             spread(
-                site_col[:, s, :].bitcast(F32)[:, 4 * h : 4 * h + 4],
+                site_col[:].bitcast(F32)[:, 4 * h : 4 * h + 4],
                 site_all[s][:].bitcast(F32).rearrange("p (q h j) -> p h q j", h=2, j=4)[:, h],
             )
 
@@ -249,6 +253,16 @@ def tile_capped_skill_task_fit_h1_kernel(
                 if (b + 1) % stores == 0:
                     store_y(i, b + 1 - stores, b + 1)
 
+        def v_bank(i, b):
+            weigh(i, b, v_product(i, b))
+            if b < 3 or i >= last - 1:
+                round_y(i, b)
+            if i == last:
+                store_y(i, b, b + 1)
+            elif b % 2 == 1:
+                store_y(i, b - 1, b + 1)
+
+        last = TILES - 1
         spread_skill()
         spread_site(0, 0)
         split_a(0, slice(0, 1))
@@ -266,73 +280,77 @@ def tile_capped_skill_task_fit_h1_kernel(
                 turn_a(1, 1)
             for half in range(2):
                 z_pass(0, first_banks[half], half, g)
-        split_a(2, slice(0, 2))
-        quantise_a(1, 0, 4)
+        quantise_a(1, 0, 2)
+        quantise_a(1, 2, 4)
         cap(0, 0, first_banks[0])
         cap(0, 1, first_banks[1])
+        split_a(2, slice(0, 2))
+        second_banks = [take_bank(), take_bank()]
+        for half, g in [(0, 0), (0, 1), (1, 0), (1, 1), (0, 2), (0, 3), (1, 2), (1, 3)]:
+            z_pass(1, second_banks[half], half, g)
+        cap(1, 0, second_banks[0])
+        cap(1, 1, second_banks[1])
+        turn_c(0, nc.scalar.copy)
+        quantise_c(0)
+        turn_a(2, 0)
+        turn_a(2, 1)
+        turn_c(1, nc.scalar.copy)
+        quantise_a(2, 0, 4)
+        v_bank(0, 0)
+        split_a(3, slice(0, 2))
+        for b in range(1, T_GROUPS):
+            v_bank(0, b)
 
-        def v_bank(i, b):
-            weigh(i, b, v_product(i, b))
-            if b < 3 or i >= last - 1:
-                round_y(i, b)
-            if i == last:
-                store_y(i, b, b + 1)
-            elif b % 2 == 1:
-                store_y(i, b - 1, b + 1)
-
-        last = TILES - 1
-        for s in range(last):
-            if s > 0:
+        for s in range(1, last):
+            if s > 1:
                 turn_c(s, nc.scalar.copy)
-            if 0 < s and s + 3 < TILES:
+            if s + 3 < TILES:
                 split_a(s + 3, slice(0, 2))
-            if s > 0:
-                quantise_c(s)
-            if s >= 2:
-                quantise_y(s - 2, 0, 4)
-                if s == last - 1:
-                    store_codes(s - 2, s - 1, 0, 4)
-                elif s % 2 == 1:
-                    store_codes(s - 3, s - 1, 0, 4)
+            quantise_c(s)
+            if s >= 3:
+                quantise_y(s - 3, 0, 4)
+                if s % 2 == 0:
+                    store_codes(s - 4, s - 2, 0, 4)
             if s + 2 < TILES:
                 turn_a(s + 2, 0)
                 turn_a(s + 2, 1)
-            if s == 0:
-                turn_c(s, nc.scalar.copy)
-            if s >= 1:
+            if s < last - 1:
                 round_y(s - 1, 3)
-            cap(s + 1, 0, z_product(s + 1, 0))
-            if s == 0:
-                quantise_c(s)
-                split_a(3, slice(0, 2))
+            if s >= 2:
+                turn_y(s - 2, 0, 2, nc.scalar.copy)
+                turn_y(s - 2, 2, 4, nc.scalar.copy)
+            if s == last - 1:
+                round_y(s - 1, 3)
             if s + 2 < TILES:
                 quantise_a(s + 2, 0, 4)
+            cap(s + 1, 0, z_product(s + 1, 0))
+            if s == last - 1:
+                quantise_y(s - 2, 0, 4)
+                store_codes(s - 2, s - 1, 0, 4)
             cap(s + 1, 1, z_product(s + 1, 1))
-            if s >= 1:
-                turn_y(s - 1, 0, 2, nc.scalar.copy)
-                turn_y(s - 1, 2, 4, nc.scalar.copy)
-            if s <= 5:
-                spread_site((s + 2) // 2, s % 2)
             for b in range(T_GROUPS):
                 v_bank(s, b)
+            if s in (1, 3):
+                load_site((s + 3) // 2)
 
         turn_c(last, nc.vector.tensor_copy)
-        quantise_y(last - 2, 0, 2)
+        turn_y(last - 2, 0, 2, nc.scalar.copy)
         quantise_c(last)
-        quantise_y(last - 2, 2, 4)
-        store_codes(last - 2, last - 1, 0, 4)
-        store_scales(0, last - 1, [nc.sync])
+        turn_y(last - 2, 2, 4, nc.vector.tensor_copy)
         turn_y(last - 1, 0, 2, nc.scalar.copy)
         turn_y(last - 1, 2, 4, nc.scalar.copy)
-        quantise_y(last - 1, 0, 4)
-        store_codes(last - 1, last, 0, 4)
+        quantise_y(last - 2, 0, 4)
+        store_codes(last - 2, last - 1, 0, 4)
+        store_scales(0, last - 1, [nc.sync])
         for b in range(T_GROUPS):
             v_bank(last, b)
+        quantise_y(last - 1, 0, 4)
+        store_codes(last - 1, last, 0, 4)
         turn_y(last, 0, 2, nc.vector.tensor_copy)
-        turn_y(last, 2, 3, nc.vector.tensor_copy)
-        quantise_y(last, 0, 2)
+        turn_y(last, 2, 3, nc.scalar.copy)
         turn_y(last, 3, 4, nc.scalar.copy)
         quantise_y(last, 2, 3)
+        quantise_y(last, 0, 2)
         store_codes(last, last + 1, 0, 3)
         quantise_y(last, 3, 4)
         store_codes(last, last + 1, 3, 4)

@@ -50,7 +50,7 @@ def tile_capped_skill_task_fit_h1_kernel(
 
         ident = keep.tile([P, P], F32, name="ident", align_bytes=64)
         skill_col = keep.tile([P, F // P], BF16, name="skill_col", align_bytes=64)
-        site_col = keep.tile([P, T // P], BF16, name="site_col", align_bytes=64)
+        site_col = keep.tile([P, 2, T // P], BF16, name="site_col", align_bytes=64)
         skill_all = keep.tile([P, F], BF16, name="skill_all", align_bytes=64)
         site_all = ring("site_all", G, [P, T], BF16)
         l_words = ring("l_words", W_PASSES, [P, 2 * F], U8)
@@ -68,7 +68,7 @@ def tile_capped_skill_task_fit_h1_kernel(
         c_scales = ring("c_scales", 3, [P, F // 4], U8)
         y_f32 = ring("y_f32", 4, [P, T], F32)
         y_split = ring("y_split", 2, [P, T], BF16)
-        y_grouped = ring("y_grouped", 2, [P, T], BF16)
+        y_grouped = ring("y_grouped", 2, [P, T_GROUPS, 2 * BANK], BF16)
         y_codes = keep.tile([P, T_GROUPS, ROWS], U32, name="y_codes", align_bytes=64)
         y_scales = keep.tile([P, T_GROUPS, ROWS], U8, name="y_scales", align_bytes=64)
 
@@ -87,24 +87,16 @@ def tile_capped_skill_task_fit_h1_kernel(
                 nc.sync.dma_start(out=plane[r:P:32, :, :].bitcast(I32), in_=by_row[r])
 
         nc.vector.memset(l_scales[:].bitcast(I32), 0)
-        nc.vector.memset(r_scales[:].bitcast(I32), 0)
         make_identity(nc, ident[:])
         nc.scalar.dma_start(out=skill_col[:], in_=skill_weight.rearrange("(p c) -> p c", p=P))
-        nc.scalar.dma_start(out=site_col[:], in_=site_weight[0].rearrange("(p c) -> p c", p=P))
+        nc.scalar.dma_start(out=site_col[:], in_=site_weight[0:2].rearrange("s (p c) -> p s c", p=P))
         load_a(0, 0, W // 2)
         load_a(0, W // 2, W)
-        load_scales(l_scales, skill_scales)
         for g in range(W_PASSES):
             if g == 2:
+                load_scales(l_scales, skill_scales)
                 load_a(1, 0, W)
             nc.sync.dma_start(out=l_words[g][:].bitcast(I32), in_=skill_words[g].bitcast(I32))
-        load_a(2, 0, W)
-        load_scales(r_scales, task_scales)
-        for g in range(F_PASSES):
-            nc.sync.dma_start(out=r_words[g][:].bitcast(I32), in_=task_words[g].bitcast(I32))
-        for i in range(3, TILES):
-            load_a(i, 0, W)
-        load_site(1)
 
         def spread(columns, dst):
             bank = take_bank()
@@ -117,7 +109,7 @@ def tile_capped_skill_task_fit_h1_kernel(
 
         def spread_site(s, h):
             spread(
-                site_col[:].bitcast(F32)[:, 4 * h : 4 * h + 4],
+                site_col[:, s, :].bitcast(F32)[:, 4 * h : 4 * h + 4],
                 site_all[s][:].bitcast(F32).rearrange("p (q h j) -> p h q j", h=2, j=4)[:, h],
             )
 
@@ -127,20 +119,20 @@ def tile_capped_skill_task_fit_h1_kernel(
             for c in range(n):
                 nc.tensor.transpose(bank[:, c * P : (c + 1) * P], sources[c], ident[:])
             engine_copy(
-                out=dst.bitcast(F32).rearrange("p (g r u) -> p g r u", r=P, u=2),
+                out=dst.bitcast(F32).rearrange("p g (r u) -> p g r u", u=2),
                 in_=bank[:, : n * P].rearrange("p (g u r) -> p g r u", r=P, u=2),
             )
 
-        def split_a(i, halves):
+        def split_a(i, halves, engine_copy):
             words = a_raw[i][:].bitcast(F32).rearrange("p (h q u) -> p h u q", h=2, u=2)
-            nc.vector.tensor_copy(out=pick(a_split, i)[:, halves], in_=words[:, halves])
+            engine_copy(out=pick(a_split, i)[:, halves], in_=words[:, halves])
 
-        def turn_a(i, h):
+        def turn_a(i, h, engine_copy):
             src = pick(a_split, i)
             turn(
                 [src[:, h, u, g * P : (g + 1) * P] for g in range(2) for u in range(2)],
-                pick(a_grouped, i)[:, h * 1024 : (h + 1) * 1024],
-                nc.scalar.copy,
+                pick(a_grouped, i)[:, h * 1024 : (h + 1) * 1024].rearrange("p (g c) -> p g c", g=2),
+                engine_copy,
             )
 
         def quantise(codes, scales, grouped):
@@ -181,7 +173,7 @@ def tile_capped_skill_task_fit_h1_kernel(
 
         def turn_c(i, engine_copy):
             words = pick(c_split, i)[:].bitcast(F32)
-            turn([words[:, c * P : (c + 1) * P] for c in range(4)], pick(c_grouped, i)[:], engine_copy)
+            turn([words[:, c * P : (c + 1) * P] for c in range(4)], pick(c_grouped, i)[:].rearrange("p (g c) -> p g c", g=2), engine_copy)
 
         def quantise_c(i):
             quantise(pick(c_codes, i)[:], pick(c_scales, i)[:], pick(c_grouped, i)[:])
@@ -206,11 +198,22 @@ def tile_capped_skill_task_fit_h1_kernel(
                 out=pick(y_f32, i)[:, cols], in0=bank[:], in1=site_all[i * P // SHIFTS][:, cols], op=ALU.mult
             )
 
-        def round_y(i, b):
+        def split_view(tile, lo, hi):
+            return tile[:, lo * BANK : hi * BANK].rearrange("p (u q e) -> p u q e", u=2, e=2)
+
+        def quads(ap):
+            return ap.rearrange("p (q u e) -> p u q e", u=2, e=2)
+
+        def round_y(i, lo, hi):
+            nc.scalar.copy(out=split_view(pick(y_split, i), lo, hi), in_=quads(pick(y_f32, i)[:, lo * BANK : hi * BANK]))
+
+        def weigh_rounded(i, b, bank):
             cols = slice(b * BANK, (b + 1) * BANK)
-            nc.scalar.copy(
-                out=pick(y_split, i)[:, cols].rearrange("p (u q e) -> p u q e", u=2, e=2),
-                in_=pick(y_f32, i)[:, cols].rearrange("p (q u e) -> p u q e", u=2, e=2),
+            nc.vector.tensor_tensor(
+                out=split_view(pick(y_split, i), b, b + 1),
+                in0=quads(bank[:]),
+                in1=quads(site_all[i * P // SHIFTS][:, cols]),
+                op=ALU.mult,
             )
 
         def store_y(i, lo, hi):
@@ -218,19 +221,20 @@ def tile_capped_skill_task_fit_h1_kernel(
             nc.sync.dma_start(out=y_rows[i * P : (i + 1) * P, cols], in_=pick(y_f32, i)[:, cols])
 
         def turn_y(i, lo, hi, engine_copy):
-            words = pick(y_split, i)[:].bitcast(F32)
+            span = 1 if i >= last - 1 else T_GROUPS
+            words = pick(y_split, i)[:].bitcast(F32).rearrange("p (c u g q) -> p c g u q", u=2, g=span, q=P)
             turn(
-                [words[:, c * P : (c + 1) * P] for c in range(2 * lo, 2 * hi)],
-                pick(y_grouped, i)[:, lo * BANK : hi * BANK],
+                [words[:, g // span, g % span, u, :] for g in range(lo, hi) for u in range(2)],
+                pick(y_grouped, i // 2)[:, lo:hi, (i % 2) * BANK : (i % 2 + 1) * BANK],
                 engine_copy,
             )
 
-        def quantise_y(i, lo, hi):
+        def quantise_y(pair, lo, hi):
             for g in range(lo, hi):
                 quantise(
-                    y_codes[:, g, i * P : (i + 1) * P],
-                    y_scales[:, g, i * P : (i + 1) * P],
-                    pick(y_grouped, i)[:, g * BANK : (g + 1) * BANK],
+                    y_codes[:, g, pair * 2 * P : (pair + 1) * 2 * P],
+                    y_scales[:, g, pair * 2 * P : (pair + 1) * 2 * P],
+                    pick(y_grouped, pair)[:, g, :],
                 )
 
         def store_codes(first, last, lo, hi):
@@ -246,112 +250,114 @@ def tile_capped_skill_task_fit_h1_kernel(
                     in_=y_scales[r:P:32, :, first * P : last * P].bitcast(I32),
                 )
 
-        def v_stage(i, stores):
-            for b in range(T_GROUPS):
-                weigh(i, b, v_product(i, b))
-                round_y(i, b)
-                if (b + 1) % stores == 0:
-                    store_y(i, b + 1 - stores, b + 1)
-
-        def v_bank(i, b):
-            weigh(i, b, v_product(i, b))
-            if b < 3 or i >= last - 1:
-                round_y(i, b)
-            if i == last:
-                store_y(i, b, b + 1)
-            elif b % 2 == 1:
-                store_y(i, b - 1, b + 1)
-
         last = TILES - 1
+        on_s, on_v = nc.scalar.copy, nc.vector.tensor_copy
         spread_skill()
+        split_a(0, slice(0, 1), on_v)
+        split_a(0, slice(1, 2), on_v)
+        nc.vector.memset(r_scales[:].bitcast(I32), 0)
+        load_a(2, 0, W)
+        load_scales(r_scales, task_scales)
+        for g in range(F_PASSES):
+            nc.sync.dma_start(out=r_words[g][:].bitcast(I32), in_=task_words[g].bitcast(I32))
+        for i in range(3, TILES):
+            load_a(i, 0, W)
+        load_site(2)
+        turn_a(0, 0, on_s)
+        turn_a(0, 1, on_s)
         spread_site(0, 0)
-        split_a(0, slice(0, 1))
-        split_a(0, slice(1, 2))
-        turn_a(0, 0)
-        turn_a(0, 1)
         spread_site(0, 1)
         quantise_a(0, 0, 2)
         quantise_a(0, 2, 4)
         first_banks = [take_bank(), take_bank()]
         for g in range(W_PASSES):
             if g == 2:
-                split_a(1, slice(0, 2))
-                turn_a(1, 0)
-                turn_a(1, 1)
+                split_a(1, slice(0, 2), on_v)
+                turn_a(1, 0, on_s)
+                turn_a(1, 1, on_v)
             for half in range(2):
                 z_pass(0, first_banks[half], half, g)
+        split_a(2, slice(0, 2), on_s)
         quantise_a(1, 0, 2)
         quantise_a(1, 2, 4)
         cap(0, 0, first_banks[0])
         cap(0, 1, first_banks[1])
-        split_a(2, slice(0, 2))
         second_banks = [take_bank(), take_bank()]
         for half, g in [(0, 0), (0, 1), (1, 0), (1, 1), (0, 2), (0, 3), (1, 2), (1, 3)]:
             z_pass(1, second_banks[half], half, g)
         cap(1, 0, second_banks[0])
-        cap(1, 1, second_banks[1])
-        turn_c(0, nc.scalar.copy)
+        turn_c(0, on_s)
         quantise_c(0)
-        turn_a(2, 0)
-        turn_a(2, 1)
-        turn_c(1, nc.scalar.copy)
+        cap(1, 1, second_banks[1])
+        turn_a(2, 0, on_s)
+        turn_a(2, 1, on_s)
+        split_a(3, slice(0, 2), on_s)
+        spread_site(1, 0)
+        spread_site(1, 1)
         quantise_a(2, 0, 4)
-        v_bank(0, 0)
-        split_a(3, slice(0, 2))
-        for b in range(1, T_GROUPS):
-            v_bank(0, b)
+        for b in range(T_GROUPS):
+            weigh(0, b, v_product(0, b))
+            if b % 2 == 1:
+                store_y(0, b - 1, b + 1)
 
         for s in range(1, last):
-            if s > 1:
-                turn_c(s, nc.scalar.copy)
-            if s + 3 < TILES:
-                split_a(s + 3, slice(0, 2))
+            turn_c(s, on_s)
+            if s >= 4:
+                quantise_y((s - 4) // 2, 2 * (s % 2), 2 * (s % 2) + 2)
+                store_codes(s - 4 - s % 2, s - 2 - s % 2, 2 * (s % 2), 2 * (s % 2) + 2)
             quantise_c(s)
-            if s >= 3:
-                quantise_y(s - 3, 0, 4)
-                if s % 2 == 0:
-                    store_codes(s - 4, s - 2, 0, 4)
+            if s in (2, 3, 4):
+                split_a(s + 3, slice(1 if s == 4 else 0, 2), on_v)
             if s + 2 < TILES:
-                turn_a(s + 2, 0)
-                turn_a(s + 2, 1)
-            if s < last - 1:
-                round_y(s - 1, 3)
+                turn_a(s + 2, 0, on_s)
+                turn_a(s + 2, 1, on_s)
             if s >= 2:
-                turn_y(s - 2, 0, 2, nc.scalar.copy)
-                turn_y(s - 2, 2, 4, nc.scalar.copy)
-            if s == last - 1:
-                round_y(s - 1, 3)
+                turn_y(s - 2, 0, 2, on_s)
+                turn_y(s - 2, 2, 4, on_s)
+            if s in (1, 4):
+                split_a(s + 3, slice(0, 1 if s == 4 else 2), on_s)
+            round_y(s - 1, 0, 4)
             if s + 2 < TILES:
                 quantise_a(s + 2, 0, 4)
             cap(s + 1, 0, z_product(s + 1, 0))
-            if s == last - 1:
-                quantise_y(s - 2, 0, 4)
-                store_codes(s - 2, s - 1, 0, 4)
             cap(s + 1, 1, z_product(s + 1, 1))
             for b in range(T_GROUPS):
-                v_bank(s, b)
-            if s in (1, 3):
-                load_site((s + 3) // 2)
+                weigh(s, b, v_product(s, b))
+                if s == last - 1:
+                    round_y(s, b, b + 1)
+                if b % 2 == 1:
+                    store_y(s, b - 1, b + 1)
+            if s == 3:
+                load_site(3)
 
-        turn_c(last, nc.vector.tensor_copy)
-        turn_y(last - 2, 0, 2, nc.scalar.copy)
+        turn_c(last, on_v)
+        quantise_y(1, 2, 3)
+        turn_y(last - 2, 0, 2, on_s)
         quantise_c(last)
-        turn_y(last - 2, 2, 4, nc.vector.tensor_copy)
-        turn_y(last - 1, 0, 2, nc.scalar.copy)
-        turn_y(last - 1, 2, 4, nc.scalar.copy)
-        quantise_y(last - 2, 0, 4)
-        store_codes(last - 2, last - 1, 0, 4)
-        store_scales(0, last - 1, [nc.sync])
-        for b in range(T_GROUPS):
-            v_bank(last, b)
-        quantise_y(last - 1, 0, 4)
-        store_codes(last - 1, last, 0, 4)
-        turn_y(last, 0, 2, nc.vector.tensor_copy)
-        turn_y(last, 2, 3, nc.scalar.copy)
-        turn_y(last, 3, 4, nc.scalar.copy)
-        quantise_y(last, 2, 3)
-        quantise_y(last, 0, 2)
-        store_codes(last, last + 1, 0, 3)
-        quantise_y(last, 3, 4)
-        store_codes(last, last + 1, 3, 4)
-        store_scales(last - 1, TILES, [nc.scalar, nc.sync])
+        quantise_y(1, 3, 4)
+        store_codes(2, 4, 2, 4)
+        store_scales(0, 4, [nc.sync])
+        turn_y(last - 2, 2, 4, on_s)
+        turn_y(last - 1, 0, 2, on_s)
+        turn_y(last - 1, 2, 4, on_s)
+        quantise_y(2, 0, 2)
+        store_codes(4, 6, 0, 2)
+        for b in range(T_GROUPS - 1):
+            weigh(last, b, v_product(last, b))
+            round_y(last, b, b + 1)
+            store_y(last, b, b + 1)
+        bank = v_product(last, 3)
+        weigh_rounded(last, 3, bank)
+        weigh(last, 3, bank)
+        store_y(last, 3, 4)
+        quantise_y(2, 2, 4)
+        store_codes(4, 6, 2, 4)
+        turn_y(last, 0, 2, on_s)
+        turn_y(last, 2, 4, on_s)
+        quantise_y(3, 0, 2)
+        store_codes(6, 8, 0, 2)
+        quantise_y(3, 2, 3)
+        store_codes(6, 8, 2, 3)
+        quantise_y(3, 3, 4)
+        store_codes(6, 8, 3, 4)
+        store_scales(4, TILES, [nc.scalar, nc.sync])

@@ -93,7 +93,7 @@ def tile_capped_skill_task_fit_h1_kernel(
         load_a(0, 0, W // 2)
         load_a(0, W // 2, W)
         for g in range(W_PASSES):
-            if g == 2:
+            if g == 1:
                 load_scales(l_scales, skill_scales)
                 load_a(1, 0, W)
             nc.sync.dma_start(out=l_words[g][:].bitcast(I32), in_=skill_words[g].bitcast(I32))
@@ -171,12 +171,20 @@ def tile_capped_skill_task_fit_h1_kernel(
                     out=c[:, u], in0=z[:, u], scalar=1.0, in1=weight[:, u], op0=ALU.min, op1=ALU.mult
                 )
 
-        def turn_c(i, engine_copy):
+        def turn_c(i, lo, hi, engine_copy):
             words = pick(c_split, i)[:].bitcast(F32)
-            turn([words[:, c * P : (c + 1) * P] for c in range(4)], pick(c_grouped, i)[:].rearrange("p (g c) -> p g c", g=2), engine_copy)
+            turn(
+                [words[:, c * P : (c + 1) * P] for c in range(2 * lo, 2 * hi)],
+                pick(c_grouped, i)[:, lo * BANK : hi * BANK].rearrange("p (g c) -> p g c", c=BANK),
+                engine_copy,
+            )
 
-        def quantise_c(i):
-            quantise(pick(c_codes, i)[:], pick(c_scales, i)[:], pick(c_grouped, i)[:])
+        def quantise_c(i, lo, hi):
+            quantise(
+                pick(c_codes, i)[:, lo * P : hi * P],
+                pick(c_scales, i)[:, lo * P : hi * P],
+                pick(c_grouped, i)[:, lo * BANK : hi * BANK],
+            )
 
         def v_product(i, b):
             bank = take_bank()
@@ -271,11 +279,11 @@ def tile_capped_skill_task_fit_h1_kernel(
         quantise_a(0, 2, 4)
         first_banks = [take_bank(), take_bank()]
         for g in range(W_PASSES):
-            if g == 2:
-                split_a(1, slice(0, 2), on_v)
-                turn_a(1, 0, on_s)
-                turn_a(1, 1, on_v)
             for half in range(2):
+                if (g, half) == (1, 1):
+                    split_a(1, slice(0, 2), on_v)
+                    turn_a(1, 0, on_s)
+                    turn_a(1, 1, on_v)
                 z_pass(0, first_banks[half], half, g)
         split_a(2, slice(0, 2), on_s)
         quantise_a(1, 0, 2)
@@ -286,9 +294,11 @@ def tile_capped_skill_task_fit_h1_kernel(
         for half, g in [(0, 0), (0, 1), (1, 0), (1, 1), (0, 2), (0, 3), (1, 2), (1, 3)]:
             z_pass(1, second_banks[half], half, g)
         cap(1, 0, second_banks[0])
-        turn_c(0, on_s)
-        quantise_c(0)
+        turn_c(0, 0, 1, on_s)
+        turn_c(0, 1, 2, on_s)
         cap(1, 1, second_banks[1])
+        quantise_c(0, 0, 1)
+        quantise_c(0, 1, 2)
         turn_a(2, 0, on_s)
         turn_a(2, 1, on_s)
         split_a(3, slice(0, 2), on_s)
@@ -301,11 +311,11 @@ def tile_capped_skill_task_fit_h1_kernel(
                 store_y(0, b - 1, b + 1)
 
         for s in range(1, last):
-            turn_c(s, on_s)
+            turn_c(s, 0, 2, on_s)
             if s >= 4:
                 quantise_y((s - 4) // 2, 2 * (s % 2), 2 * (s % 2) + 2)
                 store_codes(s - 4 - s % 2, s - 2 - s % 2, 2 * (s % 2), 2 * (s % 2) + 2)
-            quantise_c(s)
+            quantise_c(s, 0, 2)
             if s in (2, 3, 4):
                 split_a(s + 3, slice(1 if s == 4 else 0, 2), on_v)
             if s + 2 < TILES:
@@ -330,10 +340,10 @@ def tile_capped_skill_task_fit_h1_kernel(
             if s == 3:
                 load_site(3)
 
-        turn_c(last, on_v)
+        turn_c(last, 0, 2, on_v)
         quantise_y(1, 2, 3)
         turn_y(last - 2, 0, 2, on_s)
-        quantise_c(last)
+        quantise_c(last, 0, 2)
         quantise_y(1, 3, 4)
         store_codes(2, 4, 2, 4)
         store_scales(0, 4, [nc.sync])

from contextlib import ExitStack

import concourse.mybir as mybir
from concourse.masks import make_identity

G, SHIFTS, W, F, T = 4, 256, 2048, 1024, 2048
ROWS = G * SHIFTS
FLOPS = 2 * ROWS * W * F + 2 * ROWS * F * T

F32 = mybir.dt.float32
BF16 = mybir.dt.bfloat16
I32 = mybir.dt.int32
U32 = mybir.dt.uint32
U8 = mybir.dt.uint8
FP8X4 = mybir.dt.float8_e4m3fn_x4
FP4X4 = mybir.dt.float4_e2m1fn_x4
ALU = mybir.AluOpType

P = 128
BANK = 512
TILES = ROWS // P
W_PASSES = W // 512
F_PASSES = F // 512
T_GROUPS = T // 512
BANKS = 8


def tile_capped_skill_task_fit_h1_kernel(
    tc, assign, skill_words, skill_scales, skill_weight, task_words, task_scales, site_weight, out_0, out_1, out_2
):
    nc = tc.nc
    a_rows = assign.rearrange("s j w -> (s j) w")
    y_rows = out_0.rearrange("s j d -> (s j) d")
    y_words = out_1.rearrange("g p m t -> p g (m t)").bitcast(I32)

    with ExitStack() as ctx:
        keep = ctx.enter_context(tc.tile_pool(name="keep", bufs=1))
        psum = ctx.enter_context(tc.psum_pool(name="psum", bufs=1))
        ctx.enter_context(tc.manual_schedule())

        def ring(label, count, shape, dtype):
            return [keep.tile(shape, dtype, name="%s%d" % (label, n), align_bytes=64) for n in range(count)]

        banks = [psum.tile([P, BANK], F32, name="bank%d" % n) for n in range(BANKS)]
        bank_uses = []

        def take_bank():
            bank_uses.append(None)
            return banks[(len(bank_uses) - 1) % BANKS]

        ident = keep.tile([P, P], F32, name="ident", align_bytes=64)
        skill_col = keep.tile([P, F // P], BF16, name="skill_col", align_bytes=64)
        site_col = keep.tile([P, 2, T // P], BF16, name="site_col", align_bytes=64)
        skill_all = keep.tile([P, F], BF16, name="skill_all", align_bytes=64)
        site_all = ring("site_all", G, [P, T], BF16)
        l_words = ring("l_words", W_PASSES, [P, 2 * F], U8)
        r_words = ring("r_words", F_PASSES, [P, 2 * T], U8)
        l_scales = keep.tile([P, W_PASSES, F], U8, name="l_scales", align_bytes=64)
        r_scales = keep.tile([P, F_PASSES, T], U8, name="r_scales", align_bytes=64)
        a_raw = ring("a_raw", TILES, [P, W], BF16)
        a_split = ring("a_split", 2, [P, 2, 2, W // 8], F32)
        a_grouped = ring("a_grouped", 2, [P, W], BF16)
        a_codes = ring("a_codes", 3, [P, W // 4], U32)
        a_scales = ring("a_scales", 3, [P, W // 4], U8)
        c_split = ring("c_split", 2, [P, F], BF16)
        c_grouped = ring("c_grouped", 2, [P, F], BF16)
        c_codes = ring("c_codes", 3, [P, F // 4], U32)
        c_scales = ring("c_scales", 3, [P, F // 4], U8)
        y_f32 = ring("y_f32", 4, [P, T], F32)
        y_split = ring("y_split", 2, [P, T], BF16)
        y_grouped = ring("y_grouped", 2, [P, T_GROUPS, 2 * BANK], BF16)
        y_codes = keep.tile([P, T_GROUPS, ROWS], U32, name="y_codes", align_bytes=64)
        y_scales = keep.tile([P, T_GROUPS, ROWS], U8, name="y_scales", align_bytes=64)

        def pick(tiles, i):
            return tiles[i % len(tiles)]

        def load_a(i, lo, hi):
            nc.sync.dma_start(out=a_raw[i][:, lo:hi], in_=a_rows[i * P : (i + 1) * P, lo:hi])

        def load_site(s):
            nc.sync.dma_start(out=site_all[s][:], in_=site_weight[s].partition_broadcast(P))

        def load_scales(plane, rows):
            by_row = rows.rearrange("g (q r) n -> r q g n", r=4).bitcast(I32)
            for r in range(4):
                nc.sync.dma_start(out=plane[r:P:32, :, :].bitcast(I32), in_=by_row[r])

        nc.vector.memset(l_scales[:].bitcast(I32), 0)
        make_identity(nc, ident[:])
        nc.scalar.dma_start(out=skill_col[:], in_=skill_weight.rearrange("(p c) -> p c", p=P))
        nc.scalar.dma_start(out=site_col[:], in_=site_weight[0:2].rearrange("s (p c) -> p s c", p=P))
        load_a(0, 0, W // 2)
        load_a(0, W // 2, W)
        for g in range(W_PASSES):
            if g == 1:
                load_scales(l_scales, skill_scales)
                load_a(1, 0, W)
            nc.sync.dma_start(out=l_words[g][:].bitcast(I32), in_=skill_words[g].bitcast(I32))

        def spread(columns, dst):
            bank = take_bank()
            for j in range(4):
                nc.tensor.transpose(bank[:, j * P : (j + 1) * P], columns[:, j : j + 1].to_broadcast([P, P]), ident[:])
            nc.scalar.copy(out=dst, in_=bank[:].rearrange("p (j q) -> p q j", j=4))

        def spread_skill():
            spread(skill_col[:].bitcast(F32), skill_all[:].bitcast(F32).rearrange("p (q j) -> p q j", j=4))

        def spread_site(s, h):
            spread(
                site_col[:, s, :].bitcast(F32)[:, 4 * h : 4 * h + 4],
                site_all[s][:].bitcast(F32).rearrange("p (q h j) -> p h q j", h=2, j=4)[:, h],
            )

        def turn(sources, dst, engine_copy):
            bank = take_bank()
            n = len(sources)
            for c in range(n):
                nc.tensor.transpose(bank[:, c * P : (c + 1) * P], sources[c], ident[:])
            engine_copy(
                out=dst.bitcast(F32).rearrange("p g (r u) -> p g r u", u=2),
                in_=bank[:, : n * P].rearrange("p (g u r) -> p g r u", r=P, u=2),
            )

        def split_a(i, halves, engine_copy):
            words = a_raw[i][:].bitcast(F32).rearrange("p (h q u) -> p h u q", h=2, u=2)
            engine_copy(out=pick(a_split, i)[:, halves], in_=words[:, halves])

        def turn_a(i, h, engine_copy):
            src = pick(a_split, i)
            turn(
                [src[:, h, u, g * P : (g + 1) * P] for g in range(2) for u in range(2)],
                pick(a_grouped, i)[:, h * 1024 : (h + 1) * 1024].rearrange("p (g c) -> p g c", g=2),
                engine_copy,
            )

        def quantise(codes, scales, grouped):
            nc.vector.quantize_mx(out=codes.bitcast(FP8X4), scales=scales, in_=grouped)

        def quantise_a(i, lo, hi):
            quantise(
                pick(a_codes, i)[:, lo * P : hi * P],
                pick(a_scales, i)[:, lo * P : hi * P],
                pick(a_grouped, i)[:, lo * BANK : hi * BANK],
            )

        def z_pass(i, bank, half, g):
            nc.tensor.matmul_mx(
                out=bank[:],
                lhsT=pick(a_codes, i)[:, g * P : (g + 1) * P].bitcast(FP8X4),
                lhsT_scale=pick(a_scales, i)[:, g * P : (g + 1) * P],
                rhs=l_words[g][:, half * 2 * BANK : (half + 1) * 2 * BANK].bitcast(FP4X4),
                rhs_scale=l_scales[:, g, half * BANK : (half + 1) * BANK],
                start=(g == 0),
                stop=(g == W_PASSES - 1),
            )

        def z_product(i, half):
            bank = take_bank()
            for g in range(W_PASSES):
                z_pass(i, bank, half, g)
            return bank

        def cap(i, half, bank):
            z = bank[:].rearrange("p (q u e) -> p u q e", u=2, e=2)
            weight = skill_all[:, half * BANK : (half + 1) * BANK].rearrange("p (q u e) -> p u q e", u=2, e=2)
            c = pick(c_split, i)[:, half * BANK : (half + 1) * BANK].rearrange("p (u q e) -> p u q e", u=2, e=2)
            for u in range(2):
                nc.vector.scalar_tensor_tensor(
                    out=c[:, u], in0=z[:, u], scalar=1.0, in1=weight[:, u], op0=ALU.min, op1=ALU.mult
                )

        def turn_c(i, lo, hi, engine_copy):
            words = pick(c_split, i)[:].bitcast(F32)
            turn(
                [words[:, c * P : (c + 1) * P] for c in range(2 * lo, 2 * hi)],
                pick(c_grouped, i)[:, lo * BANK : hi * BANK].rearrange("p (g c) -> p g c", c=BANK),
                engine_copy,
            )

        def quantise_c(i, lo, hi):
            quantise(
                pick(c_codes, i)[:, lo * P : hi * P],
                pick(c_scales, i)[:, lo * P : hi * P],
                pick(c_grouped, i)[:, lo * BANK : hi * BANK],
            )

        def v_product(i, b):
            bank = take_bank()
            for g in range(F_PASSES):
                nc.tensor.matmul_mx(
                    out=bank[:],
                    lhsT=pick(c_codes, i)[:, g * P : (g + 1) * P].bitcast(FP8X4),
                    lhsT_scale=pick(c_scales, i)[:, g * P : (g + 1) * P],
                    rhs=r_words[g][:, b * 2 * BANK : (b + 1) * 2 * BANK].bitcast(FP4X4),
                    rhs_scale=r_scales[:, g, b * BANK : (b + 1) * BANK],
                    start=(g == 0),
                    stop=(g == F_PASSES - 1),
                )
            return bank

        def weigh(i, b, bank):
            cols = slice(b * BANK, (b + 1) * BANK)
            nc.vector.tensor_tensor(
                out=pick(y_f32, i)[:, cols], in0=bank[:], in1=site_all[i * P // SHIFTS][:, cols], op=ALU.mult
            )

        def split_view(tile, lo, hi):
            return tile[:, lo * BANK : hi * BANK].rearrange("p (u q e) -> p u q e", u=2, e=2)

        def quads(ap):
            return ap.rearrange("p (q u e) -> p u q e", u=2, e=2)

        def round_y(i, lo, hi):
            nc.scalar.copy(out=split_view(pick(y_split, i), lo, hi), in_=quads(pick(y_f32, i)[:, lo * BANK : hi * BANK]))

        def weigh_rounded(i, b, bank):
            cols = slice(b * BANK, (b + 1) * BANK)
            nc.vector.tensor_tensor(
                out=split_view(pick(y_split, i), b, b + 1),
                in0=quads(bank[:]),
                in1=quads(site_all[i * P // SHIFTS][:, cols]),
                op=ALU.mult,
            )

        def store_y(i, lo, hi):
            cols = slice(lo * BANK, hi * BANK)
            nc.sync.dma_start(out=y_rows[i * P : (i + 1) * P, cols], in_=pick(y_f32, i)[:, cols])

        def turn_y(i, lo, hi, engine_copy):
            span = 1 if i >= last - 1 else T_GROUPS
            words = pick(y_split, i)[:].bitcast(F32).rearrange("p (c u g q) -> p c g u q", u=2, g=span, q=P)
            turn(
                [words[:, g // span, g % span, u, :] for g in range(lo, hi) for u in range(2)],
                pick(y_grouped, i // 2)[:, lo:hi, (i % 2) * BANK : (i % 2 + 1) * BANK],
                engine_copy,
            )

        def quantise_y(pair, lo, hi):
            for g in range(lo, hi):
                quantise(
                    y_codes[:, g, pair * 2 * P : (pair + 1) * 2 * P],
                    y_scales[:, g, pair * 2 * P : (pair + 1) * 2 * P],
                    pick(y_grouped, pair)[:, g, :],
                )

        def store_codes(first, last, lo, hi):
            nc.sync.dma_start(
                out=y_words[:, lo:hi, first * P : last * P], in_=y_codes[:, lo:hi, first * P : last * P].bitcast(I32)
            )

        def store_scales(first, last, queues):
            by_row = out_2.rearrange("g (q r) m -> r q g m", r=4)
            for r in range(4):
                queues[r % len(queues)].dma_start(
                    out=by_row[r][:, :, first * P : last * P].bitcast(I32),
                    in_=y_scales[r:P:32, :, first * P : last * P].bitcast(I32),
                )

        last = TILES - 1
        on_s, on_v = nc.scalar.copy, nc.vector.tensor_copy
        spread_skill()
        split_a(0, slice(0, 1), on_v)
        split_a(0, slice(1, 2), on_v)
        nc.vector.memset(r_scales[:].bitcast(I32), 0)
        load_a(2, 0, W)
        load_scales(r_scales, task_scales)
        for g in range(F_PASSES):
            nc.sync.dma_start(out=r_words[g][:].bitcast(I32), in_=task_words[g].bitcast(I32))
        for i in range(3, TILES):
            load_a(i, 0, W)
        load_site(2)
        turn_a(0, 0, on_s)
        turn_a(0, 1, on_s)
        spread_site(0, 0)
        spread_site(0, 1)
        quantise_a(0, 0, 2)
        quantise_a(0, 2, 4)
        first_banks = [take_bank(), take_bank()]
        for g in range(W_PASSES):
            for half in range(2):
                if (g, half) == (1, 1):
                    split_a(1, slice(0, 2), on_v)
                    turn_a(1, 0, on_s)
                    turn_a(1, 1, on_v)
                z_pass(0, first_banks[half], half, g)
        split_a(2, slice(0, 2), on_s)
        quantise_a(1, 0, 2)
        quantise_a(1, 2, 4)
        cap(0, 0, first_banks[0])
        cap(0, 1, first_banks[1])
        second_banks = [take_bank(), take_bank()]
        for half, g in [(0, 0), (0, 1), (1, 0), (1, 1), (0, 2), (0, 3), (1, 2), (1, 3)]:
            z_pass(1, second_banks[half], half, g)
        cap(1, 0, second_banks[0])
        turn_c(0, 0, 1, on_s)
        turn_c(0, 1, 2, on_s)
        cap(1, 1, second_banks[1])
        quantise_c(0, 0, 1)
        quantise_c(0, 1, 2)
        turn_a(2, 0, on_s)
        turn_a(2, 1, on_s)
        split_a(3, slice(0, 2), on_s)
        spread_site(1, 0)
        spread_site(1, 1)
        quantise_a(2, 0, 4)
        for b in range(T_GROUPS):
            weigh(0, b, v_product(0, b))
            if b % 2 == 1:
                store_y(0, b - 1, b + 1)

        for s in range(1, last):
            turn_c(s, 0, 2, on_s)
            if s >= 4:
                quantise_y((s - 4) // 2, 2 * (s % 2), 2 * (s % 2) + 2)
                store_codes(s - 4 - s % 2, s - 2 - s % 2, 2 * (s % 2), 2 * (s % 2) + 2)
            quantise_c(s, 0, 2)
            if s in (2, 3, 4):
                split_a(s + 3, slice(1 if s == 4 else 0, 2), on_v)
            if s + 2 < TILES:
                turn_a(s + 2, 0, on_s)
                turn_a(s + 2, 1, on_s)
            if s >= 2:
                turn_y(s - 2, 0, 2, on_s)
                turn_y(s - 2, 2, 4, on_s)
            if s in (1, 4):
                split_a(s + 3, slice(0, 1 if s == 4 else 2), on_s)
            round_y(s - 1, 0, 4)
            if s + 2 < TILES:
                quantise_a(s + 2, 0, 4)
            cap(s + 1, 0, z_product(s + 1, 0))
            cap(s + 1, 1, z_product(s + 1, 1))
            for b in range(T_GROUPS):
                weigh(s, b, v_product(s, b))
                if s == last - 1:
                    round_y(s, b, b + 1)
                if b % 2 == 1:
                    store_y(s, b - 1, b + 1)
            if s == 3:
                load_site(3)

        turn_c(last, 0, 2, on_v)
        quantise_y(1, 2, 3)
        turn_y(last - 2, 0, 2, on_s)
        quantise_c(last, 0, 2)
        quantise_y(1, 3, 4)
        store_codes(2, 4, 2, 4)
        store_scales(0, 4, [nc.sync])
        turn_y(last - 2, 2, 4, on_s)
        turn_y(last - 1, 0, 2, on_s)
        turn_y(last - 1, 2, 4, on_s)
        quantise_y(2, 0, 2)
        store_codes(4, 6, 0, 2)
        for b in range(T_GROUPS - 1):
            weigh(last, b, v_product(last, b))
            round_y(last, b, b + 1)
            store_y(last, b, b + 1)
        bank = v_product(last, 3)
        weigh_rounded(last, 3, bank)
        weigh(last, 3, bank)
        store_y(last, 3, 4)
        quantise_y(2, 2, 4)
        store_codes(4, 6, 2, 4)
        turn_y(last, 0, 2, on_s)
        turn_y(last, 2, 4, on_s)
        quantise_y(3, 0, 2)
        store_codes(6, 8, 0, 2)
        quantise_y(3, 2, 3)
        store_codes(6, 8, 2, 3)
        quantise_y(3, 3, 4)
        store_codes(6, 8, 3, 4)
        store_scales(4, TILES, [nc.scalar, nc.sync])
